import numpy as np
import ml_dtypes


def mxq(x, axis, fmt="e4m3"):
    dtype, down = {"e4m3": (ml_dtypes.float8_e4m3fn, 7), "e5m2": (ml_dtypes.float8_e5m2, 14)}[fmt]
    v = np.moveaxis(np.asarray(x, np.float32).astype(ml_dtypes.bfloat16).astype(np.float64), axis, -1)
    blocks = v.reshape(v.shape[:-1] + (-1, 32))
    amax = np.abs(blocks).max(-1, keepdims=True)
    byte = np.maximum(np.where(amax > 0, np.frexp(amax)[1] - 1 + 127, 0) - down, 1)
    scale = np.exp2(byte - 127.0)
    codes = (blocks / scale).astype(np.float32).astype(dtype).astype(np.float64)
    return np.moveaxis((codes * scale).reshape(v.shape), -1, axis)


WIDE = False


def mx_kscale(k):
    if not WIDE:
        return np.ones(k)
    levels = np.array([10, -10, 5, -5, 0])
    if k % 512:
        return np.exp2(np.random.permutation(np.resize(levels, k // 32))).repeat(32)
    a = np.empty((k // 512, 16))
    for p in range(k // 512):
        a[p, :8] = np.random.permutation(np.resize(levels, 8))
        for g in range(8):
            far = levels[np.abs(levels - a[p, g]) >= 10]
            a[p, g + 8] = far[np.random.randint(len(far))]
    return np.exp2(a.ravel()).repeat(32)


def f64(x):
    return np.asarray(x).astype(np.float64)


def striped(idx):
    return np.tile(idx.reshape(-1, 16).T, (8, 1)).astype(np.uint16)


def unstriped(offs):
    return offs[:16].T.reshape(-1).astype(np.int64)


def striped8(idx):
    return np.concatenate([x.reshape(-1, 16).T for x in idx]).astype(np.uint16)


def runs(offs, k):
    lists = np.stack([offs[16 * r : 16 * r + 16].T.reshape(-1) for r in range(8)]).astype(np.int64)
    return lists[np.arange(k) % 512 // 64]


def pack_weight(w):
    k, n = w.shape
    w = f64(np.asarray(w, np.float32).astype(ml_dtypes.bfloat16)).reshape(k // 32, 32, n)
    amax = np.abs(w).max(1)
    byte = np.clip(np.where(amax > 0, np.frexp(amax)[1] - 1 + 127 - 7, 1), 1, 254)
    scaled = (w * np.exp2(127.0 - byte)[:, None, :]).reshape(k, n).astype(np.float32)
    words = np.ascontiguousarray(scaled.reshape(k // 512, 128, 4, n).transpose(0, 1, 3, 2)).astype(ml_dtypes.float8_e4m3fn).view(np.uint8)
    return words, np.ascontiguousarray(byte.astype(np.uint8).reshape(k // 512, 16, n))


def unpack_weight(words, scales):
    g, p, n, _ = words.shape
    vals = np.ascontiguousarray(words).view(ml_dtypes.float8_e4m3fn).astype(np.float64) * np.repeat(np.exp2(scales.astype(np.float64) - 127.0), 8, axis=1)[..., None]
    return vals.transpose(0, 1, 3, 2).reshape(g * 512, n)


K, T, S, H, W, G, U = 512, 2048, 512, 512, 256, 2048, 1024


def setup_inputs():
    n = np.random.standard_normal
    s = mx_kscale(K)[:, None]
    packed_xT = pack_weight(n((K, T)) * s)
    packed_dT = pack_weight(n((K, G)) / s)
    perm = np.stack([np.random.permutation(U) for _ in range(8)])
    return {
        "x_words": packed_xT[0],
        "x_scales": packed_xT[1],
        "w1": (n((K, H)) / np.sqrt(K) / s).astype(np.float32),
        "gs": (np.random.uniform(0.5, 1.5, (K, 1)) * s).astype(np.float32),
        "d_words": packed_dT[0],
        "d_scales": packed_dT[1],
        "offs": striped(np.random.permutation(T)[:S]),
        "n1": striped8(np.stack([np.random.permutation(S)[:W] for _ in range(8)])),
        "n2": striped8(np.stack([np.random.permutation(S)[:W] for _ in range(8)])),
        "n3": striped8(np.stack([np.random.permutation(S) for _ in range(8)])),
        "k1": striped8(np.random.randint(0, G, (8, H))),
        "n4": striped8(perm[:, :S]),
        "n5": striped8(perm[:, S:]),
        "n6": striped8(np.stack([np.random.permutation(U) for _ in range(8)])),
    }


def reference(x_words, x_scales, w1, gs, d_words, d_scales, offs, n1, n2, n3, k1, n4, n5, n6):
    d_k1 = unpack_weight(d_words, d_scales)[np.arange(K)[:, None], runs(k1, K)]
    xq = unpack_weight(x_words, x_scales)[:, unstriped(offs)]
    y = mxq(f64(w1), 0, "e4m3").T @ xq
    pa = y[np.arange(H)[:, None], runs(n2, H)]
    ds = y.copy()
    ds[np.arange(H)[:, None], runs(n1, H)] = pa
    z = f64(gs) * (ds - (0.5 * (ds[np.arange(H)[:, None], runs(n3, H)])))
    h = 0.0625 * ((d_k1.T @ mxq(z, 0, "e4m3")))
    nw = 0.5 * h
    ph = np.zeros((H, U))
    ph[np.arange(H)[:, None], runs(n4, H)] = h
    pg = ph.copy()
    pg[np.arange(H)[:, None], runs(n5, H)] = nw
    return pg - (pg[np.arange(H)[:, None], runs(n6, H)])

@@ -1,0 +1,186 @@
+from contextlib import ExitStack
+
+import concourse.mybir as mybir
+
+F32 = mybir.dt.float32
+BF16 = mybir.dt.bfloat16
+U32 = mybir.dt.uint32
+I32 = mybir.dt.int32
+U16 = mybir.dt.uint16
+U8 = mybir.dt.uint8
+FP8X4 = mybir.dt.float8_e4m3fn_x4
+COPY = mybir.ActivationFunctionType.Copy
+ADD = mybir.AluOpType.add
+SUB = mybir.AluOpType.subtract
+
+P = 128
+K, T, S, H, W, G, U = 512, 2048, 512, 512, 256, 2048, 1024
+HALF = S // 2
+W_SPLIT = 80
+FLOPS = 2 * K * H * S + 2 * K * H * S
+
+
+def tile_picked_denseksetpagtwo_none_p_kernel(tc, x_words, x_scales, w1, gs, d_words, d_scales, offs, n1, n2, n3, k1, n4, n5, n6, out):
+    nc = tc.nc
+    with ExitStack() as ctx:
+        keep = ctx.enter_context(tc.tile_pool(name="keep", bufs=1))
+        psum = ctx.enter_context(tc.psum_pool(name="psum", bufs=1))
+
+        def load_list(src, name):
+            tile = keep.tile(list(src.shape), U16, name=name)
+            nc.sync.dma_start(tile[:], src)
+            return tile
+
+        def entries(tile, first, count):
+            return tile[:, first // 16 : (first + count) // 16]
+
+        xs_table = keep.tile([P, T], U8, name="xs_table")
+        nc.vector.memset(xs_table[:].bitcast(I32), 0)
+        ds_table = keep.tile([P, G], U8, name="ds_table")
+        nc.vector.memset(ds_table[:].bitcast(I32), 0)
+        d_plane = keep.tile([P, H], U8, name="d_plane", align_bytes=64)
+        nc.vector.memset(d_plane[:].bitcast(I32), 0)
+
+        offs_t = load_list(offs, "offs_t")
+        w_raw = keep.tile([P, 4, H], F32, name="w_raw")
+        nc.sync.dma_start(w_raw[:], w1.rearrange("(p j) c -> p j c", j=4))
+        for q in range(4):
+            nc.sync.dma_start(xs_table[32 * q : 32 * q + 4, :].bitcast(I32), x_scales[0, 4 * q : 4 * q + 4, :].bitcast(I32))
+        xw_table = keep.tile([P, T], U32, name="xw_table")
+        nc.sync.dma_start(xw_table[:].bitcast(I32), x_words[0].rearrange("p n r -> p (n r)").bitcast(I32))
+        k1_t = load_list(k1, "k1_t")
+        nc.sync.dma_start(ds_table[0:P:8, :].bitcast(I32), d_scales[0].bitcast(I32))
+        gs_t = keep.tile([P, 4], F32, name="gs_t")
+        nc.sync.dma_start(gs_t[:], gs.rearrange("(p t) o -> p (t o)", t=4))
+        n2_t = load_list(n2, "n2_t")
+        n1_t = load_list(n1, "n1_t")
+        n3_t = load_list(n3, "n3_t")
+        dw_table = keep.tile([P, G], U32, name="dw_table")
+        nc.sync.dma_start(dw_table[:].bitcast(I32), d_words[0].rearrange("p n r -> p (n r)").bitcast(I32))
+        n4_t = load_list(n4, "n4_t")
+        n5_t = load_list(n5, "n5_t")
+        n6_t = load_list(n6, "n6_t")
+
+        x_plane = keep.tile([P, S], U8, name="x_plane", align_bytes=64)
+        nc.vector.tensor_copy(x_plane[:], xs_table[:].indirect(offs_t[:]))
+        w_bf = keep.tile([P, 4, P, 4], BF16, name="w_bf", align_bytes=64)
+        w_to = w_bf[:].rearrange("p t m j -> p m j t")
+        w_from = w_raw[:].rearrange("p j (m t) -> p m j t", t=4)
+        nc.vector.tensor_copy(w_to[:, :W_SPLIT], w_from[:, :W_SPLIT])
+        nc.scalar.copy(w_to[:, W_SPLIT:], w_from[:, W_SPLIT:])
+        w_codes = keep.tile([P, H], U32, name="w_codes", align_bytes=64)
+        w_plane = keep.tile([P, H], U8, name="w_plane", align_bytes=64)
+        nc.vector.quantize_mx(out=w_codes[:].bitcast(FP8X4), scales=w_plane[:], in_=w_bf[:].rearrange("p t m j -> p (t m j)"))
+        x_codes = keep.tile([P, S], U32, name="x_codes", align_bytes=64)
+        nc.vector.tensor_copy(x_codes[:], xw_table[:].indirect(offs_t[:]))
+
+        d_bytes = keep.tile([P, H], U8, name="d_bytes")
+        nc.vector.tensor_copy(d_bytes[:], ds_table[:].indirect(k1_t[:]))
+        d_dealt = keep.tile([P, 4, P], U8, name="d_dealt")
+        nc.vector.tensor_copy(d_dealt[:].rearrange("p t m -> p m t"), d_bytes[:].rearrange("p (m t) -> p m t", t=4))
+        for q in range(4):
+            nc.sync.dma_start(d_plane[32 * q : 32 * q + 4, :].bitcast(I32), d_dealt[32 * q : 32 * q + 32 : 8].rearrange("p t m -> p (t m)").bitcast(I32))
+
+        rows = []
+        pulled = {}
+        halves = [slice(a * HALF, (a + 1) * HALF) for a in range(2)]
+
+        def pull(t, a):
+            pulled[t, a] = keep.tile([P, HALF], F32, name=f"pulled{t}_{a}")
+            nc.scalar.activation(pulled[t, a][:], rows[t][:].indirect(entries(n3_t, a * HALF, HALF)), COPY, scale=-0.5)
+
+        for t in range(4):
+            cols = slice(t * P, (t + 1) * P)
+            acc = psum.tile([P, S], F32, name=f"bank{t}")
+            nc.tensor.matmul_mx(out=acc[:], lhsT=w_codes[:, cols].bitcast(FP8X4), lhsT_scale=w_plane[:, cols],
+                                rhs=x_codes[:].bitcast(FP8X4), rhs_scale=x_plane[:], start=True, stop=True)
+            row = keep.tile([P, S], F32, name=f"row{t}")
+            pa = keep.tile([P, W], F32, name=f"pa{t}")
+            if t == 3:
+                pull(0, 0)
+            nc.scalar.activation(row[:], acc[:], COPY, scale=gs_t[:, t : t + 1])
+            nc.scalar.activation(pa[:], row[:].indirect(n2_t[:]), COPY)
+            nc.vector.tensor_copy(row[:].indirect(n1_t[:]), pa[:])
+            rows.append(row)
+
+        d_picked = keep.tile([P, H], U32, name="d_picked", tag="pa3")
+        nc.vector.tensor_copy(d_picked[:], dw_table[:].indirect(k1_t[:]))
+        d_codes = keep.tile([P, 4, P], U32, name="d_codes", align_bytes=64)
+        nc.vector.tensor_copy(d_codes[:].rearrange("p t m -> p m t"), d_picked[:].rearrange("p (m t) -> p m t", t=4))
+
+        z_bf = [keep.tile([P, HALF, 4], BF16, name=f"z_bf{a}", align_bytes=64) for a in range(2)]
+        for t, a in [(1, 0), (2, 0), (3, 0), (0, 1), (1, 1), (2, 1), (3, 1)]:
+            pull(t, a)
+        for t, a in [(0, 0), (1, 0), (2, 0), (3, 0), (0, 1), (1, 1), (2, 1), (3, 1)]:
+            nc.gpsimd.tensor_tensor(z_bf[a][:, :, t], rows[t][:, halves[a]], pulled[t, a][:], ADD)
+
+        z_codes = keep.tile([P, S], U32, name="z_codes", align_bytes=64)
+        z_plane = keep.tile([P, S], U8, name="z_plane", align_bytes=64)
+        for a in range(2):
+            nc.vector.quantize_mx(out=z_codes[:, halves[a]].bitcast(FP8X4), scales=z_plane[:, halves[a]], in_=z_bf[a][:].rearrange("p c t -> p (c t)"))
+
+        whole = slice(0, S)
+        h = [keep.tile([P, S], F32, name=f"h{t}") for t in range(4)]
+        nw = [keep.tile([P, S], F32, name=f"nw{t}") for t in range(4)]
+        pages = [keep.tile([P, U], F32, name=f"page{t}") for t in range(4)]
+        pieces = [(0, halves[0]), (1, halves[0]), (0, halves[1]), (1, halves[1]), (2, whole), (3, whole)]
+        sums = {t: [] for t in range(4)}
+        for i, (t, cols) in enumerate(pieces):
+            acc = psum.tile([P, cols.stop - cols.start], F32, name=f"bank{(4 + i) % 8}")
+            nc.tensor.matmul_mx(out=acc[:], lhsT=d_codes[:, t, :].bitcast(FP8X4), lhsT_scale=d_plane[:, t * P : (t + 1) * P],
+                                rhs=z_codes[:, cols].bitcast(FP8X4), rhs_scale=z_plane[:, cols], start=True, stop=True)
+            sums[t].append((cols, acc))
+
+        def full(t, i):
+            cols, acc = sums[t][i]
+            nc.scalar.activation(h[t][:, cols], acc[:], COPY, scale=0.0625)
+
+        def halved(t):
+            for cols, acc in sums[t]:
+                nc.scalar.activation(nw[t][:, cols], acc[:], COPY, scale=0.03125)
+
+        def put_full(t, i):
+            cols = sums[t][i][0]
+            nc.vector.tensor_copy(pages[t][:].indirect(entries(n4_t, cols.start, cols.stop - cols.start)), h[t][:, cols])
+
+        def put_halved(t):
+            nc.vector.tensor_copy(pages[t][:].indirect(n5_t[:]), nw[t][:])
+
+        for t, i in [(0, 0), (1, 0), (0, 1), (1, 1)]:
+            full(t, i)
+            put_full(t, i)
+        halved(0)
+        put_halved(0)
+        full(2, 0)
+        put_full(2, 0)
+        halved(1)
+        put_halved(1)
+        halved(2)
+        put_halved(2)
+        full(3, 0)
+        put_full(3, 0)
+        halved(3)
+        put_halved(3)
+
+        out_rows = out.rearrange("(p t) w -> t p w", t=4)
+        for t in range(4):
+            page = pages[t]
+            if t < 3:
+                for a in range(2):
+                    cols = slice(a * S, (a + 1) * S)
+                    other = keep.tile([P, S], F32, name=f"other{t}_{a}")
+                    nc.scalar.activation(other[:], page[:].indirect(entries(n6_t, a * S, S)), COPY)
+                    res = keep.tile([P, S], F32, name=f"res{t}_{a}")
+                    nc.gpsimd.tensor_tensor(res[:], page[:, cols], other[:], SUB)
+                    nc.sync.dma_start(out_rows[t][:, cols], res[:])
+            else:
+                for a in range(4):
+                    cols = slice(a * W, (a + 1) * W)
+                    other = keep.tile([P, W], F32, name=f"other{t}_{a}")
+                    if a % 2 == 0:
+                        nc.scalar.activation(other[:], page[:].indirect(entries(n6_t, a * W, W)), COPY)
+                    else:
+                        nc.vector.tensor_copy(other[:], page[:].indirect(entries(n6_t, a * W, W)))
+                    res = keep.tile([P, W], F32, name=f"res{t}_{a}")
+                    (nc.gpsimd if a == 0 else nc.vector).tensor_tensor(res[:], page[:, cols], other[:], SUB)
+                    nc.sync.dma_start(out_rows[t][:, cols], res[:])

@@ -24,6 +24,7 @@ def tile_picked_denseksetpagtwo_none_p_kernel(tc, x_words, x_scales, w1, gs, d_w
     nc = tc.nc
     with ExitStack() as ctx:
         keep = ctx.enter_context(tc.tile_pool(name="keep", bufs=1))
+        again = ctx.enter_context(tc.tile_pool(name="again", bufs=1))
         psum = ctx.enter_context(tc.psum_pool(name="psum", bufs=1))
 
         def load_list(src, name):
@@ -72,7 +73,9 @@ def tile_picked_denseksetpagtwo_none_p_kernel(tc, x_words, x_scales, w1, gs, d_w
         w_plane = keep.tile([P, H], U8, name="w_plane", align_bytes=64)
         nc.vector.quantize_mx(out=w_codes[:].bitcast(FP8X4), scales=w_plane[:], in_=w_bf[:].rearrange("p t m j -> p (t m j)"))
         x_codes = keep.tile([P, S], U32, name="x_codes", align_bytes=64)
-        nc.vector.tensor_copy(x_codes[:], xw_table[:].indirect(offs_t[:]))
+        halves = [slice(a * HALF, (a + 1) * HALF) for a in range(2)]
+        for a in range(2):
+            nc.vector.tensor_copy(x_codes[:, halves[a]], xw_table[:].indirect(entries(offs_t, a * HALF, HALF)))
 
         d_bytes = keep.tile([P, H], U8, name="d_bytes")
         nc.vector.tensor_copy(d_bytes[:], ds_table[:].indirect(k1_t[:]))
@@ -81,85 +84,114 @@ def tile_picked_denseksetpagtwo_none_p_kernel(tc, x_words, x_scales, w1, gs, d_w
         for q in range(4):
             nc.sync.dma_start(d_plane[32 * q : 32 * q + 4, :].bitcast(I32), d_dealt[32 * q : 32 * q + 32 : 8].rearrange("p t m -> p (t m)").bitcast(I32))
 
-        rows = []
+        rows = [keep.tile([P, S], F32, name=f"row{t}") for t in range(4)]
+        first_half = keep.tile([P, 4, HALF], F32, name="first_half")
         pulled = {}
-        halves = [slice(a * HALF, (a + 1) * HALF) for a in range(2)]
 
-        def pull(t, a):
-            pulled[t, a] = keep.tile([P, HALF], F32, name=f"pulled{t}_{a}")
-            nc.scalar.activation(pulled[t, a][:], rows[t][:].indirect(entries(n3_t, a * HALF, HALF)), COPY, scale=-0.5)
+        def parts(t, a):
+            return [(0, P), (P, P)] if (t, a) == (3, 0) else [(0, HALF)]
 
-        for t in range(4):
+        def pull(t, a, into):
+            pulled[t, a] = into
+            for first, count in parts(t, a):
+                nc.scalar.activation(into[:, first : first + count], rows[t][:].indirect(entries(n3_t, a * HALF + first, count)), COPY, scale=-0.5)
+
+        def project(t, tokens, acc):
             cols = slice(t * P, (t + 1) * P)
-            acc = psum.tile([P, S], F32, name=f"bank{t}")
-            nc.tensor.matmul_mx(out=acc[:], lhsT=w_codes[:, cols].bitcast(FP8X4), lhsT_scale=w_plane[:, cols],
-                                rhs=x_codes[:].bitcast(FP8X4), rhs_scale=x_plane[:], start=True, stop=True)
-            row = keep.tile([P, S], F32, name=f"row{t}")
-            pa = keep.tile([P, W], F32, name=f"pa{t}")
-            if t == 3:
-                pull(0, 0)
-            nc.scalar.activation(row[:], acc[:], COPY, scale=gs_t[:, t : t + 1])
-            nc.scalar.activation(pa[:], row[:].indirect(n2_t[:]), COPY)
-            nc.vector.tensor_copy(row[:].indirect(n1_t[:]), pa[:])
-            rows.append(row)
+            nc.tensor.matmul_mx(out=acc, lhsT=w_codes[:, cols].bitcast(FP8X4), lhsT_scale=w_plane[:, cols],
+                                rhs=x_codes[:, tokens].bitcast(FP8X4), rhs_scale=x_plane[:, tokens], start=True, stop=True)
+            nc.scalar.activation(rows[t][:, tokens], acc, COPY, scale=gs_t[:, t : t + 1])
 
-        d_picked = keep.tile([P, H], U32, name="d_picked", tag="pa3")
+        def overwrite(t):
+            pa = keep.tile([P, W], F32, name=f"pa{t}") if t < 3 else again.tile([P, W], F32, name="pa3", offset=1536)
+            nc.scalar.activation(pa[:], rows[t][:].indirect(n2_t[:]), COPY)
+            nc.vector.tensor_copy(rows[t][:].indirect(n1_t[:]), pa[:])
+
+        for a, bank in enumerate(("single", "trio")):
+            project(0, halves[a], psum.tile([P, HALF], F32, name=bank)[:])
+        overwrite(0)
+        y_rest = psum.tile([P, 3, S], F32, name="y_rest", tag="trio")
+        project(1, slice(0, S), y_rest[:, 0, :])
+        project(2, slice(0, S), y_rest[:, 1, :])
+        overwrite(1)
+        project(3, slice(0, S), y_rest[:, 2, :])
+        overwrite(2)
+        overwrite(3)
+
+        d_picked = again.tile([P, H], U32, name="d_picked", offset=0)
         nc.vector.tensor_copy(d_picked[:], dw_table[:].indirect(k1_t[:]))
-        d_codes = keep.tile([P, 4, P], U32, name="d_codes", align_bytes=64)
-        nc.vector.tensor_copy(d_codes[:].rearrange("p t m -> p m t"), d_picked[:].rearrange("p (m t) -> p m t", t=4))
+        d_first = keep.tile([P, P], U32, name="d_first", align_bytes=64)
+        d_rest = keep.tile([P, 3, P], U32, name="d_rest", align_bytes=64)
+        d_codes = [d_first[:]] + [d_rest[:, t, :] for t in range(3)]
+        d_from = d_picked[:].rearrange("p (m t) -> p m t", t=4)
+        nc.vector.tensor_copy(d_first[:], d_from[:, :, 0])
 
         z_bf = [keep.tile([P, HALF, 4], BF16, name=f"z_bf{a}", align_bytes=64) for a in range(2)]
-        for t, a in [(1, 0), (2, 0), (3, 0), (0, 1), (1, 1), (2, 1), (3, 1)]:
-            pull(t, a)
-        for t, a in [(0, 0), (1, 0), (2, 0), (3, 0), (0, 1), (1, 1), (2, 1), (3, 1)]:
-            nc.gpsimd.tensor_tensor(z_bf[a][:, :, t], rows[t][:, halves[a]], pulled[t, a][:], ADD)
+
+        def add(t, a):
+            for first, count in parts(t, a):
+                cols = slice(first, first + count)
+                nc.gpsimd.tensor_tensor(z_bf[a][:, cols, t], rows[t][:, halves[a]][:, cols], pulled[t, a][:, cols], ADD)
 
         z_codes = keep.tile([P, S], U32, name="z_codes", align_bytes=64)
         z_plane = keep.tile([P, S], U8, name="z_plane", align_bytes=64)
-        for a in range(2):
+
+        def quantise(a):
             nc.vector.quantize_mx(out=z_codes[:, halves[a]].bitcast(FP8X4), scales=z_plane[:, halves[a]], in_=z_bf[a][:].rearrange("p c t -> p (c t)"))
 
-        whole = slice(0, S)
-        h = [keep.tile([P, S], F32, name=f"h{t}") for t in range(4)]
-        nw = [keep.tile([P, S], F32, name=f"nw{t}") for t in range(4)]
-        pages = [keep.tile([P, U], F32, name=f"page{t}") for t in range(4)]
-        pieces = [(0, halves[0]), (1, halves[0]), (0, halves[1]), (1, halves[1]), (2, whole), (3, whole)]
-        sums = {t: [] for t in range(4)}
-        for i, (t, cols) in enumerate(pieces):
-            acc = psum.tile([P, cols.stop - cols.start], F32, name=f"bank{(4 + i) % 8}")
-            nc.tensor.matmul_mx(out=acc[:], lhsT=d_codes[:, t, :].bitcast(FP8X4), lhsT_scale=d_plane[:, t * P : (t + 1) * P],
-                                rhs=z_codes[:, cols].bitcast(FP8X4), rhs_scale=z_plane[:, cols], start=True, stop=True)
-            sums[t].append((cols, acc))
+        sums, h, pages = {}, {}, {}
+        h_rest = psum.tile([P, 3, S], F32, name="h_rest", tag="trio")
+        for t in range(4):
+            sums[t, 0] = psum.tile([P, HALF], F32, name=f"bank{t}")[:]
+            sums[t, 1] = h_rest[:, t - 1, :HALF] if t else psum.tile([P, HALF], F32, name="single")[:]
 
-        def full(t, i):
-            cols, acc = sums[t][i]
-            nc.scalar.activation(h[t][:, cols], acc[:], COPY, scale=0.0625)
+        def product(t, a):
+            nc.tensor.matmul_mx(out=sums[t, a], lhsT=d_codes[t].bitcast(FP8X4), lhsT_scale=d_plane[:, t * P : (t + 1) * P],
+                                rhs=z_codes[:, halves[a]].bitcast(FP8X4), rhs_scale=z_plane[:, halves[a]], start=True, stop=True)
+            h[t, a] = keep.tile([P, HALF], F32, name=f"h{t}_{a}")
+            nc.scalar.activation(h[t, a][:], sums[t, a], COPY, scale=0.0625)
 
-        def halved(t):
-            for cols, acc in sums[t]:
-                nc.scalar.activation(nw[t][:, cols], acc[:], COPY, scale=0.03125)
-
-        def put_full(t, i):
-            cols = sums[t][i][0]
-            nc.vector.tensor_copy(pages[t][:].indirect(entries(n4_t, cols.start, cols.stop - cols.start)), h[t][:, cols])
+        def put_full(t, a):
+            nc.vector.tensor_copy(pages[t][:].indirect(entries(n4_t, a * HALF, HALF)), h[t, a][:])
 
         def put_halved(t):
-            nc.vector.tensor_copy(pages[t][:].indirect(n5_t[:]), nw[t][:])
+            nw = keep.tile([P, S], F32, name=f"nw{t}")
+            for a in range(2):
+                nc.scalar.activation(nw[:, halves[a]], sums[t, a], COPY, scale=0.03125)
+            nc.vector.tensor_copy(pages[t][:].indirect(n5_t[:]), nw[:])
 
-        for t, i in [(0, 0), (1, 0), (0, 1), (1, 1)]:
-            full(t, i)
-            put_full(t, i)
-        halved(0)
-        put_halved(0)
-        full(2, 0)
-        put_full(2, 0)
-        halved(1)
-        put_halved(1)
-        halved(2)
-        put_halved(2)
-        full(3, 0)
+        for t in range(4):
+            pull(t, 0, first_half[:, t, :])
+        for t in range(4):
+            add(t, 0)
+        quantise(0)
+        nc.vector.tensor_copy(d_rest[:].rearrange("p t m -> p m t"), d_from[:, :, 1:])
+        early = again.tile([P, 2, HALF], F32, name="early", offset=2048)
+        for t in range(2):
+            pull(t, 1, early[:, t, :])
+            add(t, 1)
+        for t in range(4):
+            product(t, 0)
+        for t in range(3):
+            pages[t] = keep.tile([P, U], F32, name=f"page{t}")
+            put_full(t, 0)
+        late = keep.tile([P, 2, HALF], F32, name="late", tag="h0_0")
+        for t in range(2, 4):
+            pull(t, 1, late[:, t - 2, :])
+            add(t, 1)
+        quantise(1)
+        pages[3] = keep.tile([P, U], F32, name="page3", tag="z_bf1", align_bytes=64)
         put_full(3, 0)
-        halved(3)
+        for t in range(2):
+            product(t, 1)
+            put_full(t, 1)
+        put_halved(0)
+        product(2, 1)
+        put_full(2, 1)
+        put_halved(1)
+        put_halved(2)
+        product(3, 1)
+        put_full(3, 1)
         put_halved(3)
 
         out_rows = out.rearrange("(p t) w -> t p w", t=4)

@@ -17,6 +17,7 @@ P = 128
 K, T, S, H, W, G, U = 512, 2048, 512, 512, 256, 2048, 1024
 HALF = S // 2
 W_SPLIT = 80
+BANK = 2048
 FLOPS = 2 * K * H * S + 2 * K * H * S
 
 
@@ -107,14 +108,16 @@ def tile_picked_denseksetpagtwo_none_p_kernel(tc, x_words, x_scales, w1, gs, d_w
             nc.scalar.activation(pa[:], rows[t][:].indirect(n2_t[:]), COPY)
             nc.vector.tensor_copy(rows[t][:].indirect(n1_t[:]), pa[:])
 
-        for a, bank in enumerate(("single", "trio")):
-            project(0, halves[a], psum.tile([P, HALF], F32, name=bank)[:])
+        def bank(name, first, width):
+            return psum.tile([P, width], F32, name=name, offset=first * BANK)[:]
+
+        project(0, halves[0], bank("y0_0", 0, HALF))
+        project(0, halves[1], bank("y0_1", 1, 3 * S)[:, :HALF])
         overwrite(0)
-        y_rest = psum.tile([P, 3, S], F32, name="y_rest", tag="trio")
-        project(1, slice(0, S), y_rest[:, 0, :])
-        project(2, slice(0, S), y_rest[:, 1, :])
+        project(1, slice(0, S), bank("y1", 1, S))
+        project(2, slice(0, S), bank("y2", 2, S))
         overwrite(1)
-        project(3, slice(0, S), y_rest[:, 2, :])
+        project(3, slice(0, S), bank("y3", 3, S))
         overwrite(2)
         overwrite(3)
 
@@ -140,12 +143,9 @@ def tile_picked_denseksetpagtwo_none_p_kernel(tc, x_words, x_scales, w1, gs, d_w
             nc.vector.quantize_mx(out=z_codes[:, halves[a]].bitcast(FP8X4), scales=z_plane[:, halves[a]], in_=z_bf[a][:].rearrange("p c t -> p (c t)"))
 
         sums, h, pages = {}, {}, {}
-        h_rest = psum.tile([P, 3, S], F32, name="h_rest", tag="trio")
-        for t in range(4):
-            sums[t, 0] = psum.tile([P, HALF], F32, name=f"bank{t}")[:]
-            sums[t, 1] = h_rest[:, t - 1, :HALF] if t else psum.tile([P, HALF], F32, name="single")[:]
 
         def product(t, a):
+            sums[t, a] = bank(f"sums{t}_{a}", 4 * (1 - a) + t, HALF)
             nc.tensor.matmul_mx(out=sums[t, a], lhsT=d_codes[t].bitcast(FP8X4), lhsT_scale=d_plane[:, t * P : (t + 1) * P],
                                 rhs=z_codes[:, halves[a]].bitcast(FP8X4), rhs_scale=z_plane[:, halves[a]], start=True, stop=True)
             h[t, a] = keep.tile([P, HALF], F32, name=f"h{t}_{a}")

@@ -18,6 +18,7 @@ K, T, S, H, W, G, U = 512, 2048, 512, 512, 256, 2048, 1024
 HALF = S // 2
 W_SPLIT = 80
 BANK = 2048
+FULL, HALVED = 0.0625, 0.03125
 FLOPS = 2 * K * H * S + 2 * K * H * S
 
 
@@ -142,23 +143,22 @@ def tile_picked_denseksetpagtwo_none_p_kernel(tc, x_words, x_scales, w1, gs, d_w
         def quantise(a):
             nc.vector.quantize_mx(out=z_codes[:, halves[a]].bitcast(FP8X4), scales=z_plane[:, halves[a]], in_=z_bf[a][:].rearrange("p c t -> p (c t)"))
 
-        sums, h, pages = {}, {}, {}
+        whole = slice(0, S)
+        h = [keep.tile([P, S], F32, name=f"h{t}") for t in range(4)]
+        nw = [keep.tile([P, S], F32, name=f"nw{t}") for t in range(4)]
+        pages = {}
 
-        def product(t, a):
-            sums[t, a] = bank(f"sums{t}_{a}", 4 * (1 - a) + t, HALF)
-            nc.tensor.matmul_mx(out=sums[t, a], lhsT=d_codes[t].bitcast(FP8X4), lhsT_scale=d_plane[:, t * P : (t + 1) * P],
-                                rhs=z_codes[:, halves[a]].bitcast(FP8X4), rhs_scale=z_plane[:, halves[a]], start=True, stop=True)
-            h[t, a] = keep.tile([P, HALF], F32, name=f"h{t}_{a}")
-            nc.scalar.activation(h[t, a][:], sums[t, a], COPY, scale=0.0625)
+        def product(t, tokens, first_bank):
+            acc = bank(f"sums{t}_{tokens.start}", first_bank, tokens.stop - tokens.start)
+            nc.tensor.matmul_mx(out=acc, lhsT=d_codes[t].bitcast(FP8X4), lhsT_scale=d_plane[:, t * P : (t + 1) * P],
+                                rhs=z_codes[:, tokens].bitcast(FP8X4), rhs_scale=z_plane[:, tokens], start=True, stop=True)
+            return acc
 
-        def put_full(t, a):
-            nc.vector.tensor_copy(pages[t][:].indirect(entries(n4_t, a * HALF, HALF)), h[t, a][:])
+        def scaled(into, acc, factor):
+            nc.scalar.activation(into, acc, COPY, scale=factor)
 
-        def put_halved(t):
-            nw = keep.tile([P, S], F32, name=f"nw{t}")
-            for a in range(2):
-                nc.scalar.activation(nw[:, halves[a]], sums[t, a], COPY, scale=0.03125)
-            nc.vector.tensor_copy(pages[t][:].indirect(n5_t[:]), nw[:])
+        def put(t, slots, tokens, values):
+            nc.vector.tensor_copy(pages[t][:].indirect(entries(slots, tokens.start, tokens.stop - tokens.start)), values)
 
         for t in range(4):
             pull(t, 0, first_half[:, t, :])
@@ -170,49 +170,61 @@ def tile_picked_denseksetpagtwo_none_p_kernel(tc, x_words, x_scales, w1, gs, d_w
         for t in range(2):
             pull(t, 1, early[:, t, :])
             add(t, 1)
-        for t in range(4):
-            product(t, 0)
-        for t in range(3):
+        first, second = halves
+        sums = [product(t, first, 4 + t) for t in range(3)]
+        opening = keep.tile([P, HALF], F32, name="opening")
+        scaled(opening[:], sums[0], FULL)
+        scaled(h[1][:, first], sums[1], FULL)
+        scaled(nw[0][:, first], sums[0], HALVED)
+        for t in range(2):
             pages[t] = keep.tile([P, U], F32, name=f"page{t}")
-            put_full(t, 0)
-        late = keep.tile([P, 2, HALF], F32, name="late", tag="h0_0")
+        put(0, n4_t, first, opening[:])
+        put(1, n4_t, first, h[1][:, first])
+        put(0, n5_t, first, nw[0][:, first])
+        late = keep.tile([P, 2, HALF], F32, name="late", tag="opening")
         for t in range(2, 4):
             pull(t, 1, late[:, t - 2, :])
             add(t, 1)
+        scaled(h[2][:, first], sums[2], FULL)
+        for t in range(1, 3):
+            scaled(nw[t][:, first], sums[t], HALVED)
         quantise(1)
-        pages[3] = keep.tile([P, U], F32, name="page3", tag="z_bf1", align_bytes=64)
-        put_full(3, 0)
-        for t in range(2):
-            product(t, 1)
-            put_full(t, 1)
-        put_halved(0)
-        product(2, 1)
-        put_full(2, 1)
-        put_halved(1)
-        put_halved(2)
-        product(3, 1)
-        put_full(3, 1)
-        put_halved(3)
+        pages[2] = keep.tile([P, U], F32, name="page2", tag="z_bf1", align_bytes=64)
+        put(2, n4_t, first, h[2][:, first])
+        sums = [product(t, second, t) for t in range(3)]
+        last_sums = product(3, whole, 7)
+        scaled(h[0][:, second], sums[0], FULL)
+        scaled(h[1][:, second], sums[1], FULL)
+        scaled(nw[0][:, second], sums[0], HALVED)
+        scaled(h[2][:, second], sums[2], FULL)
+        scaled(nw[1][:, second], sums[1], HALVED)
+        scaled(h[3][:], last_sums, FULL)
+        scaled(nw[2][:, second], sums[2], HALVED)
+        scaled(nw[3][:], last_sums, HALVED)
 
         out_rows = out.rearrange("(p t) w -> t p w", t=4)
-        for t in range(4):
-            page = pages[t]
-            if t < 3:
-                for a in range(2):
-                    cols = slice(a * S, (a + 1) * S)
-                    other = keep.tile([P, S], F32, name=f"other{t}_{a}")
-                    nc.scalar.activation(other[:], page[:].indirect(entries(n6_t, a * S, S)), COPY)
-                    res = keep.tile([P, S], F32, name=f"res{t}_{a}")
-                    nc.gpsimd.tensor_tensor(res[:], page[:, cols], other[:], SUB)
-                    nc.sync.dma_start(out_rows[t][:, cols], res[:])
-            else:
-                for a in range(4):
-                    cols = slice(a * W, (a + 1) * W)
-                    other = keep.tile([P, W], F32, name=f"other{t}_{a}")
-                    if a % 2 == 0:
-                        nc.scalar.activation(other[:], page[:].indirect(entries(n6_t, a * W, W)), COPY)
-                    else:
-                        nc.vector.tensor_copy(other[:], page[:].indirect(entries(n6_t, a * W, W)))
-                    res = keep.tile([P, W], F32, name=f"res{t}_{a}")
-                    (nc.gpsimd if a == 0 else nc.vector).tensor_tensor(res[:], page[:, cols], other[:], SUB)
-                    nc.sync.dma_start(out_rows[t][:, cols], res[:])
+
+        def finish(t, engine, res, pieces):
+            other = keep.tile([P, U], F32, name=f"other{t}")
+            width = U // pieces
+            for i in range(pieces):
+                cols = slice(i * width, (i + 1) * width)
+                nc.scalar.activation(other[:, cols], pages[t][:].indirect(entries(n6_t, cols.start, width)), COPY)
+                engine.tensor_tensor(res[i], pages[t][:, cols], other[:, cols], SUB)
+                nc.sync.dma_start(out_rows[t][:, cols], res[i])
+
+        pages[3] = keep.tile([P, U], F32, name="page3")
+        put(0, n4_t, second, h[0][:, second])
+        put(1, n4_t, second, h[1][:, second])
+        put(0, n5_t, second, nw[0][:, second])
+        put(2, n4_t, second, h[2][:, second])
+        put(1, n5_t, whole, nw[1][:])
+        put(3, n4_t, whole, h[3][:])
+        put(2, n5_t, whole, nw[2][:])
+        put(3, n5_t, whole, nw[3][:])
+        for t in range(2):
+            finish(t, nc.gpsimd, [keep.tile([P, S], F32, name=f"res{t}_{a}")[:] for a in range(2)], 2)
+        res2 = keep.tile([P, 2, S], F32, name="res2", tag="res1_0")
+        finish(2, nc.vector, [res2[:, a, :] for a in range(2)], 2)
+        res3 = keep.tile([P, 4, W], F32, name="res3", tag="other2")
+        finish(3, nc.vector, [res3[:, i, :] for i in range(4)], 4)

from contextlib import ExitStack

import concourse.mybir as mybir

F32 = mybir.dt.float32
BF16 = mybir.dt.bfloat16
U32 = mybir.dt.uint32
I32 = mybir.dt.int32
U16 = mybir.dt.uint16
U8 = mybir.dt.uint8
FP8X4 = mybir.dt.float8_e4m3fn_x4
COPY = mybir.ActivationFunctionType.Copy
ADD = mybir.AluOpType.add
SUB = mybir.AluOpType.subtract

P = 128
K, T, S, H, W, G, U = 512, 2048, 512, 512, 256, 2048, 1024
HALF = S // 2
W_SPLIT = 80
BANK = 2048
FULL, HALVED = 0.0625, 0.03125
FLOPS = 2 * K * H * S + 2 * K * H * S


def tile_picked_denseksetpagtwo_none_p_kernel(tc, x_words, x_scales, w1, gs, d_words, d_scales, offs, n1, n2, n3, k1, n4, n5, n6, out):
    nc = tc.nc
    with ExitStack() as ctx:
        keep = ctx.enter_context(tc.tile_pool(name="keep", bufs=1))
        again = ctx.enter_context(tc.tile_pool(name="again", bufs=1))
        psum = ctx.enter_context(tc.psum_pool(name="psum", bufs=1))

        def load_list(src, name):
            tile = keep.tile(list(src.shape), U16, name=name)
            nc.sync.dma_start(tile[:], src)
            return tile

        def entries(tile, first, count):
            return tile[:, first // 16 : (first + count) // 16]

        xs_table = keep.tile([P, T], U8, name="xs_table")
        nc.vector.memset(xs_table[:].bitcast(I32), 0)
        ds_table = keep.tile([P, G], U8, name="ds_table")
        nc.vector.memset(ds_table[:].bitcast(I32), 0)
        d_plane = keep.tile([P, H], U8, name="d_plane", align_bytes=64)
        nc.vector.memset(d_plane[:].bitcast(I32), 0)

        offs_t = load_list(offs, "offs_t")
        w_raw = keep.tile([P, 4, H], F32, name="w_raw")
        nc.sync.dma_start(w_raw[:], w1.rearrange("(p j) c -> p j c", j=4))
        for q in range(4):
            nc.sync.dma_start(xs_table[32 * q : 32 * q + 4, :].bitcast(I32), x_scales[0, 4 * q : 4 * q + 4, :].bitcast(I32))
        xw_table = keep.tile([P, T], U32, name="xw_table")
        nc.sync.dma_start(xw_table[:].bitcast(I32), x_words[0].rearrange("p n r -> p (n r)").bitcast(I32))
        k1_t = load_list(k1, "k1_t")
        nc.sync.dma_start(ds_table[0:P:8, :].bitcast(I32), d_scales[0].bitcast(I32))
        gs_t = keep.tile([P, 4], F32, name="gs_t")
        nc.sync.dma_start(gs_t[:], gs.rearrange("(p t) o -> p (t o)", t=4))
        n2_t = load_list(n2, "n2_t")
        n1_t = load_list(n1, "n1_t")
        n3_t = load_list(n3, "n3_t")
        dw_table = keep.tile([P, G], U32, name="dw_table")
        nc.sync.dma_start(dw_table[:].bitcast(I32), d_words[0].rearrange("p n r -> p (n r)").bitcast(I32))
        n4_t = load_list(n4, "n4_t")
        n5_t = load_list(n5, "n5_t")
        n6_t = load_list(n6, "n6_t")

        x_plane = keep.tile([P, S], U8, name="x_plane", align_bytes=64)
        nc.vector.tensor_copy(x_plane[:], xs_table[:].indirect(offs_t[:]))
        w_bf = keep.tile([P, 4, P, 4], BF16, name="w_bf", align_bytes=64)
        w_to = w_bf[:].rearrange("p t m j -> p m j t")
        w_from = w_raw[:].rearrange("p j (m t) -> p m j t", t=4)
        nc.vector.tensor_copy(w_to[:, :W_SPLIT], w_from[:, :W_SPLIT])
        nc.scalar.copy(w_to[:, W_SPLIT:], w_from[:, W_SPLIT:])
        w_codes = keep.tile([P, H], U32, name="w_codes", align_bytes=64)
        w_plane = keep.tile([P, H], U8, name="w_plane", align_bytes=64)
        nc.vector.quantize_mx(out=w_codes[:].bitcast(FP8X4), scales=w_plane[:], in_=w_bf[:].rearrange("p t m j -> p (t m j)"))
        x_codes = keep.tile([P, S], U32, name="x_codes", align_bytes=64)
        halves = [slice(a * HALF, (a + 1) * HALF) for a in range(2)]
        for a in range(2):
            nc.vector.tensor_copy(x_codes[:, halves[a]], xw_table[:].indirect(entries(offs_t, a * HALF, HALF)))

        d_bytes = keep.tile([P, H], U8, name="d_bytes")
        nc.vector.tensor_copy(d_bytes[:], ds_table[:].indirect(k1_t[:]))
        d_dealt = keep.tile([P, 4, P], U8, name="d_dealt")
        nc.vector.tensor_copy(d_dealt[:].rearrange("p t m -> p m t"), d_bytes[:].rearrange("p (m t) -> p m t", t=4))
        for q in range(4):
            nc.sync.dma_start(d_plane[32 * q : 32 * q + 4, :].bitcast(I32), d_dealt[32 * q : 32 * q + 32 : 8].rearrange("p t m -> p (t m)").bitcast(I32))

        rows = [keep.tile([P, S], F32, name=f"row{t}") for t in range(4)]
        first_half = keep.tile([P, 4, HALF], F32, name="first_half")
        pulled = {}

        def parts(t, a):
            return [(0, P), (P, P)] if (t, a) == (3, 0) else [(0, HALF)]

        def pull(t, a, into):
            pulled[t, a] = into
            for first, count in parts(t, a):
                nc.scalar.activation(into[:, first : first + count], rows[t][:].indirect(entries(n3_t, a * HALF + first, count)), COPY, scale=-0.5)

        def project(t, tokens, acc):
            cols = slice(t * P, (t + 1) * P)
            nc.tensor.matmul_mx(out=acc, lhsT=w_codes[:, cols].bitcast(FP8X4), lhsT_scale=w_plane[:, cols],
                                rhs=x_codes[:, tokens].bitcast(FP8X4), rhs_scale=x_plane[:, tokens], start=True, stop=True)
            nc.scalar.activation(rows[t][:, tokens], acc, COPY, scale=gs_t[:, t : t + 1])

        def overwrite(t):
            pa = keep.tile([P, W], F32, name=f"pa{t}") if t < 3 else again.tile([P, W], F32, name="pa3", offset=1536)
            nc.scalar.activation(pa[:], rows[t][:].indirect(n2_t[:]), COPY)
            nc.vector.tensor_copy(rows[t][:].indirect(n1_t[:]), pa[:])

        def bank(name, first, width):
            return psum.tile([P, width], F32, name=name, offset=first * BANK)[:]

        project(0, halves[0], bank("y0_0", 0, HALF))
        project(0, halves[1], bank("y0_1", 1, 3 * S)[:, :HALF])
        overwrite(0)
        project(1, slice(0, S), bank("y1", 1, S))
        project(2, slice(0, S), bank("y2", 2, S))
        overwrite(1)
        project(3, slice(0, S), bank("y3", 3, S))
        overwrite(2)
        overwrite(3)

        d_picked = again.tile([P, H], U32, name="d_picked", offset=0)
        nc.vector.tensor_copy(d_picked[:], dw_table[:].indirect(k1_t[:]))
        d_first = keep.tile([P, P], U32, name="d_first", align_bytes=64)
        d_rest = keep.tile([P, 3, P], U32, name="d_rest", align_bytes=64)
        d_codes = [d_first[:]] + [d_rest[:, t, :] for t in range(3)]
        d_from = d_picked[:].rearrange("p (m t) -> p m t", t=4)
        nc.vector.tensor_copy(d_first[:], d_from[:, :, 0])

        z_bf = [keep.tile([P, HALF, 4], BF16, name=f"z_bf{a}", align_bytes=64) for a in range(2)]

        def add(t, a):
            for first, count in parts(t, a):
                cols = slice(first, first + count)
                nc.gpsimd.tensor_tensor(z_bf[a][:, cols, t], rows[t][:, halves[a]][:, cols], pulled[t, a][:, cols], ADD)

        z_codes = keep.tile([P, S], U32, name="z_codes", align_bytes=64)
        z_plane = keep.tile([P, S], U8, name="z_plane", align_bytes=64)

        def quantise(a):
            nc.vector.quantize_mx(out=z_codes[:, halves[a]].bitcast(FP8X4), scales=z_plane[:, halves[a]], in_=z_bf[a][:].rearrange("p c t -> p (c t)"))

        whole = slice(0, S)
        h = [keep.tile([P, S], F32, name=f"h{t}") for t in range(4)]
        nw = [keep.tile([P, S], F32, name=f"nw{t}") for t in range(4)]
        pages = {}

        def product(t, tokens, first_bank):
            acc = bank(f"sums{t}_{tokens.start}", first_bank, tokens.stop - tokens.start)
            nc.tensor.matmul_mx(out=acc, lhsT=d_codes[t].bitcast(FP8X4), lhsT_scale=d_plane[:, t * P : (t + 1) * P],
                                rhs=z_codes[:, tokens].bitcast(FP8X4), rhs_scale=z_plane[:, tokens], start=True, stop=True)
            return acc

        def scaled(into, acc, factor):
            nc.scalar.activation(into, acc, COPY, scale=factor)

        def put(t, slots, tokens, values):
            nc.vector.tensor_copy(pages[t][:].indirect(entries(slots, tokens.start, tokens.stop - tokens.start)), values)

        for t in range(4):
            pull(t, 0, first_half[:, t, :])
        for t in range(4):
            add(t, 0)
        quantise(0)
        nc.vector.tensor_copy(d_rest[:].rearrange("p t m -> p m t"), d_from[:, :, 1:])
        early = again.tile([P, 2, HALF], F32, name="early", offset=2048)
        for t in range(2):
            pull(t, 1, early[:, t, :])
            add(t, 1)
        first, second = halves
        sums = [product(t, first, 4 + t) for t in range(3)]
        opening = keep.tile([P, HALF], F32, name="opening")
        scaled(opening[:], sums[0], FULL)
        scaled(h[1][:, first], sums[1], FULL)
        scaled(nw[0][:, first], sums[0], HALVED)
        for t in range(2):
            pages[t] = keep.tile([P, U], F32, name=f"page{t}")
        put(0, n4_t, first, opening[:])
        put(1, n4_t, first, h[1][:, first])
        put(0, n5_t, first, nw[0][:, first])
        late = keep.tile([P, 2, HALF], F32, name="late", tag="opening")
        for t in range(2, 4):
            pull(t, 1, late[:, t - 2, :])
            add(t, 1)
        scaled(h[2][:, first], sums[2], FULL)
        for t in range(1, 3):
            scaled(nw[t][:, first], sums[t], HALVED)
        quantise(1)
        pages[2] = keep.tile([P, U], F32, name="page2", tag="z_bf1", align_bytes=64)
        put(2, n4_t, first, h[2][:, first])
        sums = [product(t, second, t) for t in range(3)]
        last_sums = product(3, whole, 7)
        scaled(h[0][:, second], sums[0], FULL)
        scaled(h[1][:, second], sums[1], FULL)
        scaled(nw[0][:, second], sums[0], HALVED)
        scaled(h[2][:, second], sums[2], FULL)
        scaled(nw[1][:, second], sums[1], HALVED)
        scaled(h[3][:], last_sums, FULL)
        scaled(nw[2][:, second], sums[2], HALVED)
        scaled(nw[3][:], last_sums, HALVED)

        out_rows = out.rearrange("(p t) w -> t p w", t=4)

        def finish(t, engine, res, pieces):
            other = keep.tile([P, U], F32, name=f"other{t}")
            width = U // pieces
            for i in range(pieces):
                cols = slice(i * width, (i + 1) * width)
                nc.scalar.activation(other[:, cols], pages[t][:].indirect(entries(n6_t, cols.start, width)), COPY)
                engine.tensor_tensor(res[i], pages[t][:, cols], other[:, cols], SUB)
                nc.sync.dma_start(out_rows[t][:, cols], res[i])

        pages[3] = keep.tile([P, U], F32, name="page3")
        put(0, n4_t, second, h[0][:, second])
        put(1, n4_t, second, h[1][:, second])
        put(0, n5_t, second, nw[0][:, second])
        put(2, n4_t, second, h[2][:, second])
        put(1, n5_t, whole, nw[1][:])
        put(3, n4_t, whole, h[3][:])
        put(2, n5_t, whole, nw[2][:])
        put(3, n5_t, whole, nw[3][:])
        for t in range(2):
            finish(t, nc.gpsimd, [keep.tile([P, S], F32, name=f"res{t}_{a}")[:] for a in range(2)], 2)
        res2 = keep.tile([P, 2, S], F32, name="res2", tag="res1_0")
        finish(2, nc.vector, [res2[:, a, :] for a in range(2)], 2)
        res3 = keep.tile([P, 4, W], F32, name="res3", tag="other2")
        finish(3, nc.vector, [res3[:, i, :] for i in range(4)], 4)
